import numpy as np
import ml_dtypes


def mxq(x, axis, fmt="e4m3"):
    dtype, down = {"e4m3": (ml_dtypes.float8_e4m3fn, 7), "e5m2": (ml_dtypes.float8_e5m2, 14)}[fmt]
    v = np.moveaxis(np.asarray(x, np.float32).astype(ml_dtypes.bfloat16).astype(np.float64), axis, -1)
    blocks = v.reshape(v.shape[:-1] + (-1, 32))
    amax = np.abs(blocks).max(-1, keepdims=True)
    byte = np.maximum(np.where(amax > 0, np.frexp(amax)[1] - 1 + 127, 0) - down, 1)
    scale = np.exp2(byte - 127.0)
    codes = (blocks / scale).astype(np.float32).astype(dtype).astype(np.float64)
    return np.moveaxis((codes * scale).reshape(v.shape), -1, axis)


WIDE = False


def mx_kscale(k, group=512):
    if not WIDE:
        return np.ones(k)
    levels = np.array([10, -10, 5, -5, 0])
    if group != 512:
        return np.exp2(np.random.permutation(np.resize(levels, k // group))).repeat(group)
    if k % 512:
        return np.exp2(np.random.permutation(np.resize(levels, k // 32))).repeat(32)
    a = np.empty((k // 512, 16))
    for p in range(k // 512):
        a[p, :8] = np.random.permutation(np.resize(levels, 8))
        for g in range(8):
            far = levels[np.abs(levels - a[p, g]) >= 10]
            a[p, g + 8] = far[np.random.randint(len(far))]
    return np.exp2(a.ravel()).repeat(32)


def f64(x):
    return np.asarray(x).astype(np.float64)


def striped(idx):
    return np.tile(np.asarray(idx).reshape(-1, 16).T, (8, 1)).astype(np.uint16)


def unstriped(offs):
    return offs[:16].T.reshape(-1).astype(np.int64)


H, KV, D, NQ, N = 4, 2, 256, 512, 512
CAP = 2.0


def setup_inputs():
    n = np.random.standard_normal
    s = mx_kscale(D, 0)[:, None]
    u = mx_kscale(N)
    t = np.random.uniform(0.5, 2.0, N) * u
    v = n((KV, N, 128))
    return {
        "qT": (n((H, D, NQ)) * s * (0.70 / np.sqrt(D))).astype(np.float32),
        "kT": (n((KV, D, N)) / s).astype(np.float32),
        "t": t.reshape(N, 1).astype(np.float32),
        "v": (v / t[:, None]).astype(np.float32),
        "kb": (0.5 * n((N, 1))).astype(np.float32),
        "mask": (np.arange(N)[:, None] <= np.sort(np.random.randint(N // 4, N, NQ))[None, :]).astype(np.float32),
    }


def reference(qT, kT, t, v, kb, mask):
    a = np.repeat(mxq(f64(kT), 1, "e4m3"), H // KV, 0).transpose(0, 2, 1) @ mxq(f64(qT), 1, "e4m3")
    a = a + f64(kb)
    a = CAP * np.tanh(a / CAP)
    p = np.maximum(a, 0.0)
    p = p * f64(mask)
    w = p * f64(t)
    y = mxq(w, 1, "e4m3").transpose(0, 2, 1) @ np.repeat(mxq(f64(v), 1, "e4m3"), H // KV, 0)
    y = y / 16.0
    return y

@@ -1,0 +1,249 @@
+from contextlib import ExitStack
+
+import concourse.mybir as mybir
+
+H, KV, D, NQ, N, E = 4, 2, 256, 512, 512, 128
+FLOPS = 2 * H * N * NQ * D + 2 * H * NQ * N * E
+
+F32 = mybir.dt.float32
+BF16 = mybir.dt.bfloat16
+U32 = mybir.dt.uint32
+U8 = mybir.dt.uint8
+FP8X4 = mybir.dt.float8_e4m3fn_x4
+ACT = mybir.ActivationFunctionType
+ALU = mybir.AluOpType
+
+P = 128
+PACK = 4
+ROWS = 64
+COLS = 128
+HALF = 256
+HEAD_SETS = ((1, 2), (0, 3))
+
+
+def tile_rows_a_relu_kb_mask_cap_kernel(tc, qT, kT, t, v, kb, mask, out):
+    nc = tc.nc
+    with ExitStack() as ctx:
+        keep = ctx.enter_context(tc.tile_pool(name="keep", bufs=1))
+        work = ctx.enter_context(tc.tile_pool(name="work", bufs=3))
+        psum = ctx.enter_context(tc.psum_pool(name="psum", bufs=1))
+        ctx.enter_context(tc.manual_schedule())
+
+        def kept(name, shape, dtype):
+            return keep.tile(shape, dtype, name=name, align_bytes=64)
+
+        kb_raw = kept("kb_raw", [P, PACK], F32)
+        t_raw = kept("t_raw", [P, PACK], F32)
+        kb_half = kept("kb_half", [P, PACK], F32)
+        t_twice = kept("t_twice", [P, PACK], F32)
+        k_raw = kept("k_raw", [P, PACK, N], F32)
+        k_bf = [kept("k_bf%d" % b, [P, 2, COLS, PACK], BF16) for b in range(2)]
+        k_codes = [kept("k_codes%d" % b, [P, 2 * COLS], U32) for b in range(2)]
+        k_scales = [kept("k_scales%d" % b, [P, 2 * COLS], U8) for b in range(2)]
+        q_first = [kept("q_first%d" % c, [P, COLS, PACK], BF16) for c in range(2)]
+        v_raw = kept("v_raw", [P, KV, PACK, E], F32)
+        v_bf = kept("v_bf", [P, KV, E, PACK], BF16)
+        v_codes = kept("v_codes", [P, KV * E], U32)
+        v_scales = kept("v_scales", [P, KV * E], U8)
+        qa_raw = [kept("qa_raw%d" % a, [P, PACK, HALF], F32) for a in range(2)]
+        qb_raw = kept("qb_raw", [P, PACK, NQ], F32)
+        q_raw = [[qa_raw[0][:], qa_raw[1][:]], [qb_raw[:, :, :HALF], qb_raw[:, :, HALF:]]]
+        q_bf = [[kept("q_bf%d%d" % (s, a), [P, HALF, PACK], BF16) for a in range(2)] for s in range(2)]
+        q_codes = [[kept("q_codes%d%d" % (s, a), [P, HALF], U32) for a in range(2)] for s in range(2)]
+        q_scales = [[kept("q_scales%d%d" % (s, a), [P, HALF], U8) for a in range(2)] for s in range(2)]
+        mask_raw = [kept("mask_raw%d" % a, [P, PACK, HALF], F32) for a in range(2)]
+        factor = [kept("factor%d" % a, [P, PACK, HALF], F32) for a in range(2)]
+        units = [(s, a, g) for s in range(2) for a in range(2) for g in range(2)]
+        w_codes = [kept("w_codes%d" % u, [P, HALF], U32) for u in range(8)]
+        w_scales = [kept("w_scales%d" % u, [P, HALF], U8) for u in range(8)]
+        score_banks = [[psum.tile([P, NQ], F32, name="score%d%d" % (g, b)) for b in range(3)] for g in range(2)]
+        y_banks = [psum.tile([P, 4, E], F32, name="y%d" % b) for b in range(2)]
+        capped = {}
+        w_bf = {}
+
+        def score_cols(u, r, lo, hi):
+            s, a, g = units[u]
+            if u in (0, 7):
+                bank, first = lo // COLS, COLS * r
+            else:
+                bank, first = r // 2, HALF * (r % 2) + lo
+            return score_banks[g][(2 * (u // 2) + bank) % 3][:, first : first + hi - lo]
+
+        def interleave(engine, dst, src):
+            o = dst.rearrange("p (c i) j -> p c j i", i=4)
+            i = src.rearrange("p j (c i) -> p c j i", i=4)
+            if engine == "vector":
+                nc.vector.tensor_copy(out=o, in_=i)
+            else:
+                nc.scalar.copy(out=o, in_=i)
+
+        def quantise(codes, scales, src):
+            nc.vector.quantize_mx(out=codes.bitcast(FP8X4), scales=scales, in_=src)
+
+        def quantise_q(s, a):
+            quantise(q_codes[s][a][:], q_scales[s][a][:], q_bf[s][a][:].rearrange("p n j -> p (n j)"))
+
+        def scores(u, chunks=(0, 1)):
+            s, a, g = units[u]
+            rows = slice(ROWS * g, ROWS * (g + 1))
+            for r in range(PACK):
+                tokens = slice(COLS * (r % 2), COLS * (r % 2 + 1))
+                for c in chunks:
+                    cols = slice(COLS * c, COLS * (c + 1))
+                    nc.tensor.matmul_mx(
+                        out=score_cols(u, r, COLS * c, COLS * (c + 1)),
+                        lhsT=k_codes[r // 2][rows, tokens].bitcast(FP8X4),
+                        lhsT_scale=k_scales[r // 2][rows, tokens],
+                        rhs=q_codes[s][a][rows, cols].bitcast(FP8X4),
+                        rhs_scale=q_scales[s][a][rows, cols],
+                        start=True,
+                        stop=True,
+                    )
+
+        def cap(u, lo=0, hi=HALF):
+            if u not in capped:
+                capped[u] = work.tile([P, PACK, HALF], F32, name="capped", bufs=4)
+            for r in range(PACK):
+                nc.scalar.activation(
+                    out=capped[u][:, r, lo:hi], in_=score_cols(u, r, lo, hi), func=ACT.Tanh,
+                    bias=kb_half[:, r : r + 1], scale=0.5,
+                )
+
+        def weigh(u, lo=0, hi=HALF):
+            s, a, g = units[u]
+            if u not in w_bf:
+                w_bf[u] = work.tile([P, HALF, PACK], BF16, name="w_bf", align_bytes=64)
+            nc.vector.scalar_tensor_tensor(
+                out=w_bf[u][:, lo:hi, :],
+                in0=capped[u][:, :, lo:hi].rearrange("p r n -> p n r"),
+                scalar=0.0,
+                in1=factor[a][:, :, lo:hi].rearrange("p r n -> p n r"),
+                op0=ALU.max,
+                op1=ALU.mult,
+            )
+
+        def quantise_w(u, lo=0, hi=HALF):
+            quantise(w_codes[u][:, lo:hi], w_scales[u][:, lo:hi], w_bf[u][:, lo:hi, :].rearrange("p n j -> p (n j)"))
+
+        def values(u, bank, place, chunks=(0, 1)):
+            s, a, g = units[u]
+            feats = slice(E * g, E * (g + 1))
+            for c in chunks:
+                cols = slice(COLS * c, COLS * (c + 1))
+                nc.tensor.matmul_mx(
+                    out=y_banks[bank][:, place + c, :],
+                    lhsT=w_codes[u][:, cols].bitcast(FP8X4),
+                    lhsT_scale=w_scales[u][:, cols],
+                    rhs=v_codes[:, feats].bitcast(FP8X4),
+                    rhs_scale=v_scales[:, feats],
+                    start=True,
+                    stop=True,
+                )
+
+        def leave(bank, lo, hi):
+            y_sb = work.tile([P, 4, E], F32, name="y_sb", bufs=6)
+            nc.scalar.activation(out=y_sb[:, lo:hi, :], in_=y_banks[bank][:, lo:hi, :], func=ACT.Copy, scale=1.0 / 16.0)
+            return y_sb
+
+        def store(u, y_sb, place, lo=0, hi=2):
+            s, a, g = units[u]
+            h = HEAD_SETS[s][g]
+            rows = out[h, HALF * a + COLS * lo : HALF * a + COLS * hi, :]
+            nc.sync.dma_start(out=rows.rearrange("(c m) e -> m c e", m=COLS), in_=y_sb[:, place + lo : place + hi, :])
+
+        def finish_pair(u, bank):
+            values(u, bank, 0)
+            values(u + 1, bank, 2)
+            y_sb = leave(bank, 0, 4)
+            store(u, y_sb, 0)
+            store(u + 1, y_sb, 2)
+
+        nc.gpsimd.dma_start(out=kb_raw[:], in_=kb.rearrange("(p r) o -> p (r o)", r=PACK))
+        nc.gpsimd.dma_start(out=t_raw[:], in_=t.rearrange("(p r) o -> p (r o)", r=PACK))
+        nc.sync.dma_start(out=k_raw[:], in_=kT.rearrange("g (p j) n -> (g p) j n", j=PACK))
+        qa = qT[1:3].rearrange("g (p j) n -> (g p) j n", j=PACK)
+        mask_rows = mask.rearrange("(p r) n -> p r n", r=PACK)
+        for a in range(2):
+            nc.sync.dma_start(out=qa_raw[a][:], in_=qa[:, :, HALF * a : HALF * (a + 1)])
+            nc.sync.dma_start(out=mask_raw[a][:], in_=mask_rows[:, :, HALF * a : HALF * (a + 1)])
+        nc.sync.dma_start(out=qb_raw[:ROWS], in_=qT[0].rearrange("(p j) n -> p j n", j=PACK))
+        nc.sync.dma_start(out=v_raw[:], in_=v.rearrange("g (p j) e -> p g j e", j=PACK))
+
+        nc.scalar.activation(out=kb_half[:], in_=kb_raw[:], func=ACT.Copy, scale=0.5)
+        nc.scalar.activation(out=t_twice[:], in_=t_raw[:], func=ACT.Copy, scale=2.0)
+
+        k_src = k_raw[:].rearrange("p j (s b r) -> p b s j r", b=2, r=2)
+        nc.vector.tensor_copy(out=k_bf[0][:].rearrange("p r s j -> p s j r"), in_=k_src[:, 0])
+        nc.scalar.copy(out=k_bf[1][:].rearrange("p r s j -> p s j r"), in_=k_src[:, 1])
+        quantise(k_codes[0][:], k_scales[0][:], k_bf[0][:].rearrange("p r s j -> p (r s j)"))
+        interleave("vector", q_first[0][:], q_raw[0][0][:, :, :COLS])
+        interleave("scalar", q_first[1][:], q_raw[0][0][:, :, COLS:])
+        quantise(k_codes[1][:], k_scales[1][:], k_bf[1][:].rearrange("p r s j -> p (r s j)"))
+        for c in range(2):
+            cols = slice(COLS * c, COLS * (c + 1))
+            quantise(q_codes[0][0][:, cols], q_scales[0][0][:, cols], q_first[c][:].rearrange("p n j -> p (n j)"))
+        scores(0, (0,))
+        scores(0, (1,))
+        scores(1)
+        for r in range(PACK):
+            nc.vector.tensor_scalar(
+                out=factor[0][:, r, :], in0=mask_raw[0][:, r, :], scalar1=t_twice[:, r : r + 1], scalar2=None, op0=ALU.mult
+            )
+        cap(0, 0, COLS)
+        cap(0, COLS, HALF)
+        nc.scalar.dma_start(out=qb_raw[ROWS:], in_=qT[3].rearrange("(p j) n -> p j n", j=PACK))
+        weigh(0, 0, COLS)
+        interleave("vector", q_bf[0][1][:], q_raw[0][1])
+        weigh(0, COLS, HALF)
+        quantise_q(0, 1)
+        quantise_w(0)
+        cap(1)
+        scores(2)
+        scores(3)
+        for r in range(PACK):
+            nc.scalar.activation(out=factor[1][:, r, :], in_=mask_raw[1][:, r, :], func=ACT.Copy, scale=t_twice[:, r : r + 1])
+        weigh(1)
+        cap(2)
+        interleave("scalar", q_bf[1][0][:], q_raw[1][0])
+        weigh(2)
+        quantise_w(1)
+        quantise_q(1, 0)
+        quantise_w(2)
+        cap(3)
+        scores(4)
+        scores(5)
+        nc.vector.tensor_copy(
+            out=v_bf[:].rearrange("p g (c i) j -> p g c j i", i=4), in_=v_raw[:].rearrange("p g j (c i) -> p g c j i", i=4)
+        )
+        weigh(3)
+        quantise(v_codes[:], v_scales[:], v_bf[:].rearrange("p g e j -> p (g e j)"))
+        quantise_w(3)
+        cap(4)
+        interleave("scalar", q_bf[1][1][:], q_raw[1][1])
+        weigh(4)
+        quantise_q(1, 1)
+        quantise_w(4)
+        cap(5)
+        scores(6)
+        finish_pair(0, 0)
+        scores(7, (0,))
+        scores(7, (1,))
+        weigh(5)
+        cap(6)
+        cap(7, 0, COLS)
+        cap(7, COLS, HALF)
+        finish_pair(2, 1)
+        weigh(6)
+        quantise_w(5)
+        finish_pair(4, 0)
+        weigh(7, 0, COLS)
+        quantise_w(6)
+        values(6, 1, 0)
+        store(6, leave(1, 0, 2), 0)
+        weigh(7, COLS, HALF)
+        quantise_w(7, 0, COLS)
+        quantise_w(7, COLS, HALF)
+        values(7, 0, 0, (0,))
+        values(7, 1, 0, (1,))
+        store(7, leave(0, 0, 1), 0, 0, 1)
+        store(7, leave(1, 1, 2), 0, 1, 2)

@@ -158,8 +158,8 @@ def tile_rows_a_relu_kb_mask_cap_kernel(tc, qT, kT, t, v, kb, mask, out):
             store(u, y_sb, 0)
             store(u + 1, y_sb, 2)
 
-        nc.gpsimd.dma_start(out=kb_raw[:], in_=kb.rearrange("(p r) o -> p (r o)", r=PACK))
-        nc.gpsimd.dma_start(out=t_raw[:], in_=t.rearrange("(p r) o -> p (r o)", r=PACK))
+        nc.scalar.dma_start(out=kb_raw[:], in_=kb.rearrange("(p r) o -> p (r o)", r=PACK))
+        nc.scalar.dma_start(out=t_raw[:], in_=t.rearrange("(p r) o -> p (r o)", r=PACK))
         nc.sync.dma_start(out=k_raw[:], in_=kT.rearrange("g (p j) n -> (g p) j n", j=PACK))
         qa = qT[1:3].rearrange("g (p j) n -> (g p) j n", j=PACK)
         mask_rows = mask.rearrange("(p r) n -> p r n", r=PACK)
@@ -170,7 +170,6 @@ def tile_rows_a_relu_kb_mask_cap_kernel(tc, qT, kT, t, v, kb, mask, out):
         nc.sync.dma_start(out=v_raw[:], in_=v.rearrange("g (p j) e -> p g j e", j=PACK))
 
         nc.scalar.activation(out=kb_half[:], in_=kb_raw[:], func=ACT.Copy, scale=0.5)
-        nc.scalar.activation(out=t_twice[:], in_=t_raw[:], func=ACT.Copy, scale=2.0)
 
         k_src = k_raw[:].rearrange("p j (s b r) -> p b s j r", b=2, r=2)
         nc.vector.tensor_copy(out=k_bf[0][:].rearrange("p r s j -> p s j r"), in_=k_src[:, 0])
@@ -178,6 +177,7 @@ def tile_rows_a_relu_kb_mask_cap_kernel(tc, qT, kT, t, v, kb, mask, out):
         quantise(k_codes[0][:], k_scales[0][:], k_bf[0][:].rearrange("p r s j -> p (r s j)"))
         interleave("vector", q_first[0][:], q_raw[0][0][:, :, :COLS])
         interleave("scalar", q_first[1][:], q_raw[0][0][:, :, COLS:])
+        nc.scalar.activation(out=t_twice[:], in_=t_raw[:], func=ACT.Copy, scale=2.0)
         quantise(k_codes[1][:], k_scales[1][:], k_bf[1][:].rearrange("p r s j -> p (r s j)"))
         for c in range(2):
             cols = slice(COLS * c, COLS * (c + 1))
@@ -187,7 +187,7 @@ def tile_rows_a_relu_kb_mask_cap_kernel(tc, qT, kT, t, v, kb, mask, out):
         scores(1)
         for r in range(PACK):
             nc.vector.tensor_scalar(
-                out=factor[0][:, r, :], in0=mask_raw[0][:, r, :], scalar1=t_twice[:, r : r + 1], scalar2=None, op0=ALU.mult
+                out=factor[0][:, r, :], in0=mask_raw[0][:, r, :], scalar1=t_raw[:, r : r + 1], scalar2=2.0, op0=ALU.mult, op1=ALU.mult
             )
         cap(0, 0, COLS)
         cap(0, COLS, HALF)

@@ -18,14 +18,15 @@ PACK = 4
 ROWS = 64
 COLS = 128
 HALF = 256
+RUN = 2
 HEAD_SETS = ((1, 2), (0, 3))
+UNITS = ((0, 0, 0, 128), (0, 0, 128, 256), (0, 1, 0, 256), (0, 0, 256, 512), (0, 1, 256, 512), (1, 0, 0, 256), (1, 0, 256, 512), (1, 1, 0, 512))
 
 
 def tile_rows_a_relu_kb_mask_cap_kernel(tc, qT, kT, t, v, kb, mask, out):
     nc = tc.nc
     with ExitStack() as ctx:
         keep = ctx.enter_context(tc.tile_pool(name="keep", bufs=1))
-        work = ctx.enter_context(tc.tile_pool(name="work", bufs=3))
         psum = ctx.enter_context(tc.psum_pool(name="psum", bufs=1))
         ctx.enter_context(tc.manual_schedule())
 
@@ -35,129 +36,149 @@ def tile_rows_a_relu_kb_mask_cap_kernel(tc, qT, kT, t, v, kb, mask, out):
         kb_raw = kept("kb_raw", [P, PACK], F32)
         t_raw = kept("t_raw", [P, PACK], F32)
         kb_half = kept("kb_half", [P, PACK], F32)
-        t_twice = kept("t_twice", [P, PACK], F32)
         k_raw = kept("k_raw", [P, PACK, N], F32)
         k_bf = [kept("k_bf%d" % b, [P, 2, COLS, PACK], BF16) for b in range(2)]
         k_codes = [kept("k_codes%d" % b, [P, 2 * COLS], U32) for b in range(2)]
         k_scales = [kept("k_scales%d" % b, [P, 2 * COLS], U8) for b in range(2)]
-        q_first = [kept("q_first%d" % c, [P, COLS, PACK], BF16) for c in range(2)]
         v_raw = kept("v_raw", [P, KV, PACK, E], F32)
         v_bf = kept("v_bf", [P, KV, E, PACK], BF16)
         v_codes = kept("v_codes", [P, KV * E], U32)
         v_scales = kept("v_scales", [P, KV * E], U8)
         qa_raw = [kept("qa_raw%d" % a, [P, PACK, HALF], F32) for a in range(2)]
         qb_raw = kept("qb_raw", [P, PACK, NQ], F32)
-        q_raw = [[qa_raw[0][:], qa_raw[1][:]], [qb_raw[:, :, :HALF], qb_raw[:, :, HALF:]]]
-        q_bf = [[kept("q_bf%d%d" % (s, a), [P, HALF, PACK], BF16) for a in range(2)] for s in range(2)]
-        q_codes = [[kept("q_codes%d%d" % (s, a), [P, HALF], U32) for a in range(2)] for s in range(2)]
-        q_scales = [[kept("q_scales%d%d" % (s, a), [P, HALF], U8) for a in range(2)] for s in range(2)]
         mask_raw = [kept("mask_raw%d" % a, [P, PACK, HALF], F32) for a in range(2)]
-        factor = [kept("factor%d" % a, [P, PACK, HALF], F32) for a in range(2)]
-        units = [(s, a, g) for s in range(2) for a in range(2) for g in range(2)]
-        w_codes = [kept("w_codes%d" % u, [P, HALF], U32) for u in range(8)]
-        w_scales = [kept("w_scales%d" % u, [P, HALF], U8) for u in range(8)]
         score_banks = [[psum.tile([P, NQ], F32, name="score%d%d" % (g, b)) for b in range(3)] for g in range(2)]
         y_banks = [psum.tile([P, 4, E], F32, name="y%d" % b) for b in range(2)]
-        capped = {}
-        w_bf = {}
-
-        def score_cols(u, r, lo, hi):
-            s, a, g = units[u]
-            if u in (0, 7):
-                bank, first = lo // COLS, COLS * r
-            else:
-                bank, first = r // 2, HALF * (r % 2) + lo
-            return score_banks[g][(2 * (u // 2) + bank) % 3][:, first : first + hi - lo]
-
-        def interleave(engine, dst, src):
-            o = dst.rearrange("p (c i) j -> p c j i", i=4)
-            i = src.rearrange("p j (c i) -> p c j i", i=4)
-            if engine == "vector":
-                nc.vector.tensor_copy(out=o, in_=i)
-            else:
-                nc.scalar.copy(out=o, in_=i)
-
-        def quantise(codes, scales, src):
-            nc.vector.quantize_mx(out=codes.bitcast(FP8X4), scales=scales, in_=src)
-
-        def quantise_q(s, a):
-            quantise(q_codes[s][a][:], q_scales[s][a][:], q_bf[s][a][:].rearrange("p n j -> p (n j)"))
-
-        def scores(u, chunks=(0, 1)):
-            s, a, g = units[u]
-            rows = slice(ROWS * g, ROWS * (g + 1))
+        q_bf, q_mx, w_bf, w_mx, capped, places = {}, {}, {}, {}, {}, {}
+        used = [0, 0]
+        for u, (s, g, lo, hi) in enumerate(UNITS):
+            capped[u] = kept("capped%d" % u, [P, PACK, hi - lo], F32)
+            per_bank = min(2, NQ // (hi - lo))
             for r in range(PACK):
+                places[u, r] = score_banks[g][(used[g] + r // per_bank) % 3], (r % per_bank) * (hi - lo)
+            used[g] = used[g] + PACK // per_bank
+
+        def quantise(name, src, width):
+            codes = kept(name + "_codes", [P, width], U32)
+            scales = kept(name + "_scales", [P, width], U8)
+            nc.vector.quantize_mx(out=codes[:].bitcast(FP8X4), scales=scales[:], in_=src)
+            return codes, scales
+
+        def copy_on(engine, dst, src):
+            if engine == "vector":
+                nc.vector.tensor_copy(out=dst, in_=src)
+            else:
+                nc.scalar.copy(out=dst, in_=src)
+
+        def round_q(engine, s, lo, hi):
+            if s == 0:
+                src = qa_raw[lo // HALF][:, :, lo % HALF : lo % HALF + hi - lo]
+            else:
+                src = qb_raw[:, :, lo:hi]
+            q_bf[s, lo] = kept("q_bf%d_%d" % (s, lo), [P, hi - lo, PACK], BF16)
+            copy_on(engine, q_bf[s, lo][:].rearrange("p (c i) j -> p c j i", i=RUN), src.rearrange("p j (c i) -> p c j i", i=RUN))
+
+        def quantise_q(s, lo, hi):
+            codes, scales = quantise("q%d_%d" % (s, lo), q_bf[s, lo][:].rearrange("p n j -> p (n j)"), hi - lo)
+            for c in range(lo, hi, COLS):
+                q_mx[s, c] = codes[:, c - lo : c - lo + COLS], scales[:, c - lo : c - lo + COLS]
+
+        def round_v(engine):
+            copy_on(engine, v_bf[:].rearrange("p g (c i) j -> p g c j i", i=RUN), v_raw[:].rearrange("p g j (c i) -> p g c j i", i=RUN))
+
+        def quantise_v():
+            nc.vector.quantize_mx(out=v_codes[:].bitcast(FP8X4), scales=v_scales[:], in_=v_bf[:].rearrange("p g e j -> p (g e j)"))
+
+        def scores(u, rs=range(PACK)):
+            s, g, lo, hi = UNITS[u]
+            rows = slice(ROWS * g, ROWS * (g + 1))
+            for r in rs:
                 tokens = slice(COLS * (r % 2), COLS * (r % 2 + 1))
-                for c in chunks:
-                    cols = slice(COLS * c, COLS * (c + 1))
+                bank, first = places[u, r]
+                for c in range(lo, hi, COLS):
+                    codes, scales = q_mx[s, c]
                     nc.tensor.matmul_mx(
-                        out=score_cols(u, r, COLS * c, COLS * (c + 1)),
+                        out=bank[:, first + c - lo : first + c - lo + COLS],
                         lhsT=k_codes[r // 2][rows, tokens].bitcast(FP8X4),
                         lhsT_scale=k_scales[r // 2][rows, tokens],
-                        rhs=q_codes[s][a][rows, cols].bitcast(FP8X4),
-                        rhs_scale=q_scales[s][a][rows, cols],
+                        rhs=codes[rows].bitcast(FP8X4),
+                        rhs_scale=scales[rows],
                         start=True,
                         stop=True,
                     )
 
-        def cap(u, lo=0, hi=HALF):
-            if u not in capped:
-                capped[u] = work.tile([P, PACK, HALF], F32, name="capped", bufs=4)
-            for r in range(PACK):
+        def cap(u, rs=range(PACK)):
+            s, g, lo, hi = UNITS[u]
+            for r in rs:
+                bank, first = places[u, r]
                 nc.scalar.activation(
-                    out=capped[u][:, r, lo:hi], in_=score_cols(u, r, lo, hi), func=ACT.Tanh,
+                    out=capped[u][:, r, :], in_=bank[:, first : first + hi - lo], func=ACT.Tanh,
                     bias=kb_half[:, r : r + 1], scale=0.5,
                 )
 
-        def weigh(u, lo=0, hi=HALF):
-            s, a, g = units[u]
-            if u not in w_bf:
-                w_bf[u] = work.tile([P, HALF, PACK], BF16, name="w_bf", align_bytes=64)
-            nc.vector.scalar_tensor_tensor(
-                out=w_bf[u][:, lo:hi, :],
-                in0=capped[u][:, :, lo:hi].rearrange("p r n -> p n r"),
-                scalar=0.0,
-                in1=factor[a][:, :, lo:hi].rearrange("p r n -> p n r"),
-                op0=ALU.max,
-                op1=ALU.mult,
-            )
-
-        def quantise_w(u, lo=0, hi=HALF):
-            quantise(w_codes[u][:, lo:hi], w_scales[u][:, lo:hi], w_bf[u][:, lo:hi, :].rearrange("p n j -> p (n j)"))
-
-        def values(u, bank, place, chunks=(0, 1)):
-            s, a, g = units[u]
-            feats = slice(E * g, E * (g + 1))
-            for c in chunks:
-                cols = slice(COLS * c, COLS * (c + 1))
-                nc.tensor.matmul_mx(
-                    out=y_banks[bank][:, place + c, :],
-                    lhsT=w_codes[u][:, cols].bitcast(FP8X4),
-                    lhsT_scale=w_scales[u][:, cols],
-                    rhs=v_codes[:, feats].bitcast(FP8X4),
-                    rhs_scale=v_scales[:, feats],
-                    start=True,
-                    stop=True,
+        def scale(u, rs=range(PACK)):
+            for r in rs:
+                nc.vector.tensor_scalar(
+                    out=capped[u][:, r, :], in0=capped[u][:, r, :], scalar1=0.0, scalar2=t_twice[:, r : r + 1],
+                    op0=ALU.max, op1=ALU.mult,
                 )
 
-        def leave(bank, lo, hi):
-            y_sb = work.tile([P, 4, E], F32, name="y_sb", bufs=6)
-            nc.scalar.activation(out=y_sb[:, lo:hi, :], in_=y_banks[bank][:, lo:hi, :], func=ACT.Copy, scale=1.0 / 16.0)
-            return y_sb
+        def weigh(u, lo=None, hi=None):
+            s, g, first, last = UNITS[u]
+            if lo is None:
+                lo, hi = first, last
+            w_bf[s, g, lo] = kept("w_bf%d%d_%d" % (s, g, lo), [P, hi - lo, PACK], BF16)
+            nc.vector.tensor_tensor(
+                out=w_bf[s, g, lo][:].rearrange("p (c i) r -> p c r i", i=2),
+                in0=capped[u][:, :, lo - first : hi - first].rearrange("p r (c i) -> p c r i", i=2),
+                in1=mask_raw[lo // HALF][:, :, lo % HALF : lo % HALF + hi - lo].rearrange("p r (c i) -> p c r i", i=2),
+                op=ALU.mult,
+            )
 
-        def store(u, y_sb, place, lo=0, hi=2):
-            s, a, g = units[u]
-            h = HEAD_SETS[s][g]
-            rows = out[h, HALF * a + COLS * lo : HALF * a + COLS * hi, :]
-            nc.sync.dma_start(out=rows.rearrange("(c m) e -> m c e", m=COLS), in_=y_sb[:, place + lo : place + hi, :])
+        def quantise_w(u, lo=None, hi=None):
+            s, g, first, last = UNITS[u]
+            if lo is None:
+                lo, hi = first, last
+            codes, scales = quantise("w%d%d_%d" % (s, g, lo), w_bf[s, g, lo][:].rearrange("p n j -> p (n j)"), hi - lo)
+            for c in range(lo, hi, COLS):
+                w_mx[s, g, c] = codes[:, c - lo : c - lo + COLS], scales[:, c - lo : c - lo + COLS]
 
-        def finish_pair(u, bank):
-            values(u, bank, 0)
-            values(u + 1, bank, 2)
-            y_sb = leave(bank, 0, 4)
-            store(u, y_sb, 0)
-            store(u + 1, y_sb, 2)
+        def finish(bank, pieces, engine="scalar", queue=nc.sync):
+            place = 0
+            for s, g, lo, hi in pieces:
+                feats = slice(E * g, E * (g + 1))
+                for c in range(lo, hi, COLS):
+                    codes, scales = w_mx[s, g, c]
+                    nc.tensor.matmul_mx(
+                        out=y_banks[bank][:, place, :],
+                        lhsT=codes.bitcast(FP8X4),
+                        lhsT_scale=scales,
+                        rhs=v_codes[:, feats].bitcast(FP8X4),
+                        rhs_scale=v_scales[:, feats],
+                        start=True,
+                        stop=True,
+                    )
+                    place = place + 1
+            return lambda: leave(bank, pieces, place, engine, queue)
 
+        def leave(bank, pieces, count, engine, queue):
+            y_sb = kept("y_sb%d%d_%d" % pieces[0][:3], [P, count, E], F32)
+            if engine == "scalar":
+                nc.scalar.activation(out=y_sb[:], in_=y_banks[bank][:, :count, :], func=ACT.Copy, scale=1.0 / 16.0)
+            else:
+                nc.vector.tensor_scalar(out=y_sb[:], in0=y_banks[bank][:, :count, :], scalar1=1.0 / 16.0, scalar2=None, op0=ALU.mult)
+            place = 0
+            for s, g, lo, hi in pieces:
+                n = (hi - lo) // COLS
+                rows = out[HEAD_SETS[s][g], lo:hi, :]
+                queue.dma_start(out=rows.rearrange("(c m) e -> m c e", m=COLS), in_=y_sb[:, place : place + n, :])
+                place = place + n
+
+        def load_q3():
+            nc.scalar.dma_start(out=qb_raw[ROWS:], in_=qT[3].rearrange("(p j) n -> p j n", j=PACK))
+            nc.scalar.dma_start(out=v_raw[:], in_=v.rearrange("g (p j) e -> p g j e", j=PACK))
+
+        t_twice = kept("t_twice", [P, PACK], F32)
         nc.scalar.dma_start(out=kb_raw[:], in_=kb.rearrange("(p r) o -> p (r o)", r=PACK))
         nc.scalar.dma_start(out=t_raw[:], in_=t.rearrange("(p r) o -> p (r o)", r=PACK))
         nc.sync.dma_start(out=k_raw[:], in_=kT.rearrange("g (p j) n -> (g p) j n", j=PACK))
@@ -165,85 +186,91 @@ def tile_rows_a_relu_kb_mask_cap_kernel(tc, qT, kT, t, v, kb, mask, out):
         mask_rows = mask.rearrange("(p r) n -> p r n", r=PACK)
         for a in range(2):
             nc.sync.dma_start(out=qa_raw[a][:], in_=qa[:, :, HALF * a : HALF * (a + 1)])
-            nc.sync.dma_start(out=mask_raw[a][:], in_=mask_rows[:, :, HALF * a : HALF * (a + 1)])
+        nc.sync.dma_start(out=mask_raw[0][:], in_=mask_rows[:, :, :HALF])
         nc.sync.dma_start(out=qb_raw[:ROWS], in_=qT[0].rearrange("(p j) n -> p j n", j=PACK))
-        nc.sync.dma_start(out=v_raw[:], in_=v.rearrange("g (p j) e -> p g j e", j=PACK))
+        nc.sync.dma_start(out=mask_raw[1][:], in_=mask_rows[:, :, HALF:])
 
         nc.scalar.activation(out=kb_half[:], in_=kb_raw[:], func=ACT.Copy, scale=0.5)
-
         k_src = k_raw[:].rearrange("p j (s b r) -> p b s j r", b=2, r=2)
         nc.vector.tensor_copy(out=k_bf[0][:].rearrange("p r s j -> p s j r"), in_=k_src[:, 0])
         nc.scalar.copy(out=k_bf[1][:].rearrange("p r s j -> p s j r"), in_=k_src[:, 1])
-        quantise(k_codes[0][:], k_scales[0][:], k_bf[0][:].rearrange("p r s j -> p (r s j)"))
-        interleave("vector", q_first[0][:], q_raw[0][0][:, :, :COLS])
-        interleave("scalar", q_first[1][:], q_raw[0][0][:, :, COLS:])
-        nc.scalar.activation(out=t_twice[:], in_=t_raw[:], func=ACT.Copy, scale=2.0)
-        quantise(k_codes[1][:], k_scales[1][:], k_bf[1][:].rearrange("p r s j -> p (r s j)"))
-        for c in range(2):
-            cols = slice(COLS * c, COLS * (c + 1))
-            quantise(q_codes[0][0][:, cols], q_scales[0][0][:, cols], q_first[c][:].rearrange("p n j -> p (n j)"))
-        scores(0, (0,))
-        scores(0, (1,))
-        scores(1)
-        for r in range(PACK):
-            nc.vector.tensor_scalar(
-                out=factor[0][:, r, :], in0=mask_raw[0][:, r, :], scalar1=t_raw[:, r : r + 1], scalar2=2.0, op0=ALU.mult, op1=ALU.mult
-            )
-        cap(0, 0, COLS)
-        cap(0, COLS, HALF)
-        nc.scalar.dma_start(out=qb_raw[ROWS:], in_=qT[3].rearrange("(p j) n -> p j n", j=PACK))
-        weigh(0, 0, COLS)
-        interleave("vector", q_bf[0][1][:], q_raw[0][1])
-        weigh(0, COLS, HALF)
-        quantise_q(0, 1)
-        quantise_w(0)
-        cap(1)
+        nc.vector.tensor_scalar(out=t_twice[:], in0=t_raw[:], scalar1=2.0, scalar2=None, op0=ALU.mult)
+
+        def quantise_k(b):
+            nc.vector.quantize_mx(out=k_codes[b][:].bitcast(FP8X4), scales=k_scales[b][:], in_=k_bf[b][:].rearrange("p r s j -> p (r s j)"))
+
+        quantise_k(0)
+        round_q("vector", 0, 0, 128)
+        round_q("scalar", 0, 128, 256)
+        quantise_k(1)
+        quantise_q(0, 0, 128)
+        quantise_q(0, 128, 256)
+        scores(0)
+        scores(1, (0, 1))
+        load_q3()
+        round_q("vector", 0, 256, 512)
+        cap(0, (0, 1))
+        scores(1, (2, 3))
         scores(2)
-        scores(3)
-        for r in range(PACK):
-            nc.scalar.activation(out=factor[1][:, r, :], in_=mask_raw[1][:, r, :], func=ACT.Copy, scale=t_twice[:, r : r + 1])
-        weigh(1)
+        cap(0, (2, 3))
+        scale(0, (0, 1))
+        quantise_q(0, 256, 512)
+        scale(0, (2, 3))
+        cap(1)
+        scale(1, (0, 1))
+        weigh(0)
+        scale(1, (2, 3))
         cap(2)
-        interleave("scalar", q_bf[1][0][:], q_raw[1][0])
-        weigh(2)
-        quantise_w(1)
-        quantise_q(1, 0)
-        quantise_w(2)
-        cap(3)
+        scores(3)
         scores(4)
-        scores(5)
-        nc.vector.tensor_copy(
-            out=v_bf[:].rearrange("p g (c i) j -> p g c j i", i=4), in_=v_raw[:].rearrange("p g j (c i) -> p g c j i", i=4)
-        )
-        weigh(3)
-        quantise(v_codes[:], v_scales[:], v_bf[:].rearrange("p g e j -> p (g e j)"))
-        quantise_w(3)
+        quantise_w(0)
+        weigh(1)
+        scale(2)
+        cap(3)
+        quantise_w(1)
+        weigh(2)
         cap(4)
-        interleave("scalar", q_bf[1][1][:], q_raw[1][1])
-        weigh(4)
-        quantise_q(1, 1)
-        quantise_w(4)
+        round_q("scalar", 1, 0, 256)
+        round_q("scalar", 1, 256, 512)
+        scale(3)
+        quantise_w(2)
+        weigh(3)
+        quantise_q(1, 0, 256)
+        scores(5)
+        scale(4)
+        quantise_w(3)
+        quantise_q(1, 256, 512)
         cap(5)
         scores(6)
-        finish_pair(0, 0)
-        scores(7, (0,))
-        scores(7, (1,))
-        weigh(5)
+        scores(7, (0, 1, 2))
+        weigh(4)
+        scale(5)
+        quantise_w(4)
         cap(6)
-        cap(7, 0, COLS)
-        cap(7, COLS, HALF)
-        finish_pair(2, 1)
-        weigh(6)
+        round_v("scalar")
+        weigh(5)
+        scale(6)
         quantise_w(5)
-        finish_pair(4, 0)
-        weigh(7, 0, COLS)
+        quantise_v()
+        cap(7, (0,))
+        scores(7, (3,))
+        f0 = finish(0, [(0, 0, 0, 256), (0, 1, 0, 256)])
+        cap(7, (1, 2, 3))
+        f1 = finish(1, [(0, 0, 256, 512), (0, 1, 256, 512)])
+        f0()
+        f1()
+        weigh(6)
+        scale(7)
         quantise_w(6)
-        values(6, 1, 0)
-        store(6, leave(1, 0, 2), 0)
-        weigh(7, COLS, HALF)
-        quantise_w(7, 0, COLS)
-        quantise_w(7, COLS, HALF)
-        values(7, 0, 0, (0,))
-        values(7, 1, 0, (1,))
-        store(7, leave(0, 0, 1), 0, 0, 1)
-        store(7, leave(1, 1, 2), 0, 1, 2)
+        finish(0, [(1, 0, 0, 512)])()
+        weigh(7, 0, 256)
+        weigh(7, 256, 384)
+        quantise_w(7, 0, 256)
+        finish(1, [(1, 1, 0, 256)])()
+        weigh(7, 384, 512)
+        quantise_w(7, 256, 384)
+        quantise_w(7, 384, 512)
+        f2 = finish(0, [(1, 1, 256, 384)], "vector")
+        f3 = finish(1, [(1, 1, 384, 512)], "scalar", nc.scalar)
+        f2()
+        f3()

@@ -2,7 +2,7 @@ from contextlib import ExitStack
 
 import concourse.mybir as mybir
 
-H, KV, D, NQ, N, E = 4, 2, 256, 512, 512, 128
+H, D, NQ, N, E = 4, 256, 512, 512, 128
 FLOPS = 2 * H * N * NQ * D + 2 * H * NQ * N * E
 
 F32 = mybir.dt.float32
@@ -18,9 +18,17 @@ PACK = 4
 ROWS = 64
 COLS = 128
 HALF = 256
+BANK = 512
+SCORE_BANKS = 3
 RUN = 2
+CAP = 2.0
+
 HEAD_SETS = ((1, 2), (0, 3))
-UNITS = ((0, 0, 0, 128), (0, 0, 128, 256), (0, 1, 0, 256), (0, 0, 256, 512), (0, 1, 256, 512), (1, 0, 0, 256), (1, 0, 256, 512), (1, 1, 0, 512))
+
+UNITS = [(0, 0, 0, COLS), (0, 0, COLS, HALF), (0, 1, 0, HALF), (0, 0, HALF, NQ), (0, 1, HALF, NQ)] + [
+    (1, g, first, first + HALF) for first in (0, HALF) for g in range(2)
+]
+LAST_OF_FIRST_SET = 4
 
 
 def tile_rows_a_relu_kb_mask_cap_kernel(tc, qT, kT, t, v, kb, mask, out):
@@ -30,247 +38,201 @@ def tile_rows_a_relu_kb_mask_cap_kernel(tc, qT, kT, t, v, kb, mask, out):
         psum = ctx.enter_context(tc.psum_pool(name="psum", bufs=1))
         ctx.enter_context(tc.manual_schedule())
 
-        def kept(name, shape, dtype):
+        def sbuf(name, shape, dtype):
             return keep.tile(shape, dtype, name=name, align_bytes=64)
 
-        kb_raw = kept("kb_raw", [P, PACK], F32)
-        t_raw = kept("t_raw", [P, PACK], F32)
-        kb_half = kept("kb_half", [P, PACK], F32)
-        k_raw = kept("k_raw", [P, PACK, N], F32)
-        k_bf = [kept("k_bf%d" % b, [P, 2, COLS, PACK], BF16) for b in range(2)]
-        k_codes = [kept("k_codes%d" % b, [P, 2 * COLS], U32) for b in range(2)]
-        k_scales = [kept("k_scales%d" % b, [P, 2 * COLS], U8) for b in range(2)]
-        v_raw = kept("v_raw", [P, KV, PACK, E], F32)
-        v_bf = kept("v_bf", [P, KV, E, PACK], BF16)
-        v_codes = kept("v_codes", [P, KV * E], U32)
-        v_scales = kept("v_scales", [P, KV * E], U8)
-        qa_raw = [kept("qa_raw%d" % a, [P, PACK, HALF], F32) for a in range(2)]
-        qb_raw = kept("qb_raw", [P, PACK, NQ], F32)
-        mask_raw = [kept("mask_raw%d" % a, [P, PACK, HALF], F32) for a in range(2)]
-        score_banks = [[psum.tile([P, NQ], F32, name="score%d%d" % (g, b)) for b in range(3)] for g in range(2)]
-        y_banks = [psum.tile([P, 4, E], F32, name="y%d" % b) for b in range(2)]
-        q_bf, q_mx, w_bf, w_mx, capped, places = {}, {}, {}, {}, {}, {}
-        used = [0, 0]
-        for u, (s, g, lo, hi) in enumerate(UNITS):
-            capped[u] = kept("capped%d" % u, [P, PACK, hi - lo], F32)
-            per_bank = min(2, NQ // (hi - lo))
+        score_banks = [[psum.tile([P, BANK], F32, name="score%d%d" % (g, b)) for b in range(SCORE_BANKS)] for g in range(2)]
+        y_banks = [psum.tile([P, BANK // E, E], F32, name="y%d" % b) for b in range(2)]
+
+        fills = [[], []]
+        score_at = {}
+        for u, (s, g, first, end) in enumerate(UNITS):
+            width = end - first
             for r in range(PACK):
-                places[u, r] = score_banks[g][(used[g] + r // per_bank) % 3], (r % per_bank) * (hi - lo)
-            used[g] = used[g] + PACK // per_bank
+                column = r * width % BANK
+                if column == 0:
+                    fills[g].append([])
+                bank = score_banks[g][(len(fills[g]) - 1) % SCORE_BANKS]
+                score_at[u, r] = bank[:, column : column + width]
+                fills[g][-1].extend((u, r, c) for c in range(first, end, COLS))
 
-        def quantise(name, src, width):
-            codes = kept(name + "_codes", [P, width], U32)
-            scales = kept(name + "_scales", [P, width], U8)
-            nc.vector.quantize_mx(out=codes[:].bitcast(FP8X4), scales=scales[:], in_=src)
-            return codes, scales
+        q_bf, q_mx, capped, w_bf, w_mx = {}, {}, {}, {}, {}
 
-        def copy_on(engine, dst, src):
-            if engine == "vector":
-                nc.vector.tensor_copy(out=dst, in_=src)
-            else:
-                nc.scalar.copy(out=dst, in_=src)
+        def interleave(copy, dst, src):
+            copy(out=dst.rearrange("p (c i) j -> p c j i", i=RUN), in_=src.rearrange("p j (c i) -> p c j i", i=RUN))
 
-        def round_q(engine, s, lo, hi):
-            if s == 0:
-                src = qa_raw[lo // HALF][:, :, lo % HALF : lo % HALF + hi - lo]
-            else:
-                src = qb_raw[:, :, lo:hi]
-            q_bf[s, lo] = kept("q_bf%d_%d" % (s, lo), [P, hi - lo, PACK], BF16)
-            copy_on(engine, q_bf[s, lo][:].rearrange("p (c i) j -> p c j i", i=RUN), src.rearrange("p j (c i) -> p c j i", i=RUN))
+        def quantise(name, src):
+            width = src.shape[1]
+            codes = sbuf(name + "_codes", [P, width], U32)
+            scales = sbuf(name + "_scales", [P, width], U8)
+            nc.vector.quantize_mx(out=codes[:].bitcast(FP8X4), scales=scales[:], in_=src.rearrange("p n j -> p (n j)"))
+            return [(codes[:, c : c + COLS], scales[:, c : c + COLS]) for c in range(0, width, COLS)]
 
-        def quantise_q(s, lo, hi):
-            codes, scales = quantise("q%d_%d" % (s, lo), q_bf[s, lo][:].rearrange("p n j -> p (n j)"), hi - lo)
-            for c in range(lo, hi, COLS):
-                q_mx[s, c] = codes[:, c - lo : c - lo + COLS], scales[:, c - lo : c - lo + COLS]
+        def matmul(dst, stationary, moving, rows):
+            nc.tensor.matmul_mx(
+                out=dst,
+                lhsT=stationary[0][rows].bitcast(FP8X4),
+                lhsT_scale=stationary[1][rows],
+                rhs=moving[0][rows].bitcast(FP8X4),
+                rhs_scale=moving[1][rows],
+                start=True,
+                stop=True,
+            )
 
-        def round_v(engine):
-            copy_on(engine, v_bf[:].rearrange("p g (c i) j -> p g c j i", i=RUN), v_raw[:].rearrange("p g j (c i) -> p g c j i", i=RUN))
+        def round_q(copy, s, first, src):
+            q_bf[s, first] = sbuf("q_bf%d_%d" % (s, first), [P, src.shape[2], PACK], BF16)
+            interleave(copy, q_bf[s, first][:], src)
 
-        def quantise_v():
-            nc.vector.quantize_mx(out=v_codes[:].bitcast(FP8X4), scales=v_scales[:], in_=v_bf[:].rearrange("p g e j -> p (g e j)"))
+        def quantise_q(s, first):
+            for n, operand in enumerate(quantise("q%d_%d" % (s, first), q_bf[s, first][:])):
+                q_mx[s, first + COLS * n] = operand
 
-        def scores(u, rs=range(PACK)):
-            s, g, lo, hi = UNITS[u]
-            rows = slice(ROWS * g, ROWS * (g + 1))
-            for r in rs:
-                tokens = slice(COLS * (r % 2), COLS * (r % 2 + 1))
-                bank, first = places[u, r]
-                for c in range(lo, hi, COLS):
-                    codes, scales = q_mx[s, c]
-                    nc.tensor.matmul_mx(
-                        out=bank[:, first + c - lo : first + c - lo + COLS],
-                        lhsT=k_codes[r // 2][rows, tokens].bitcast(FP8X4),
-                        lhsT_scale=k_scales[r // 2][rows, tokens],
-                        rhs=codes[rows].bitcast(FP8X4),
-                        rhs_scale=scales[rows],
-                        start=True,
-                        stop=True,
-                    )
+        def scores(n):
+            for calls in zip(fills[0][n], fills[1][n]):
+                for u, r, c in calls:
+                    s, g, first, end = UNITS[u]
+                    dst = score_at[u, r][:, c - first : c - first + COLS]
+                    matmul(dst, k_mx[r], q_mx[s, c], slice(ROWS * g, ROWS * (g + 1)))
 
-        def cap(u, rs=range(PACK)):
-            s, g, lo, hi = UNITS[u]
-            for r in rs:
-                bank, first = places[u, r]
+        def cap(u):
+            s, g, first, end = UNITS[u]
+            capped[u] = sbuf("capped%d" % u, [P, PACK, end - first], F32)
+            for r in range(PACK):
                 nc.scalar.activation(
-                    out=capped[u][:, r, :], in_=bank[:, first : first + hi - lo], func=ACT.Tanh,
-                    bias=kb_half[:, r : r + 1], scale=0.5,
+                    out=capped[u][:, r, :], in_=score_at[u, r], func=ACT.Tanh, bias=kb_cap[:, r : r + 1], scale=1.0 / CAP
                 )
 
-        def scale(u, rs=range(PACK)):
-            for r in rs:
-                nc.vector.tensor_scalar(
-                    out=capped[u][:, r, :], in0=capped[u][:, r, :], scalar1=0.0, scalar2=t_twice[:, r : r + 1],
-                    op0=ALU.max, op1=ALU.mult,
-                )
+        def scale(u):
+            for r in range(PACK):
+                row = capped[u][:, r, :]
+                nc.vector.tensor_scalar(out=row, in0=row, scalar1=0.0, scalar2=t_cap[:, r : r + 1], op0=ALU.max, op1=ALU.mult)
 
-        def weigh(u, lo=None, hi=None):
-            s, g, first, last = UNITS[u]
-            if lo is None:
-                lo, hi = first, last
-            w_bf[s, g, lo] = kept("w_bf%d%d_%d" % (s, g, lo), [P, hi - lo, PACK], BF16)
+        def weigh(u, first, end):
+            offset = first - UNITS[u][2]
+            seen = mask_raw[first // HALF][:, :, first % HALF : first % HALF + end - first]
+            w_bf[u, first] = sbuf("w_bf%d_%d" % (u, first), [P, end - first, PACK], BF16)
             nc.vector.tensor_tensor(
-                out=w_bf[s, g, lo][:].rearrange("p (c i) r -> p c r i", i=2),
-                in0=capped[u][:, :, lo - first : hi - first].rearrange("p r (c i) -> p c r i", i=2),
-                in1=mask_raw[lo // HALF][:, :, lo % HALF : lo % HALF + hi - lo].rearrange("p r (c i) -> p c r i", i=2),
+                out=w_bf[u, first][:].rearrange("p (c i) r -> p c r i", i=RUN),
+                in0=capped[u][:, :, offset : offset + end - first].rearrange("p r (c i) -> p c r i", i=RUN),
+                in1=seen.rearrange("p r (c i) -> p c r i", i=RUN),
                 op=ALU.mult,
             )
 
-        def quantise_w(u, lo=None, hi=None):
-            s, g, first, last = UNITS[u]
-            if lo is None:
-                lo, hi = first, last
-            codes, scales = quantise("w%d%d_%d" % (s, g, lo), w_bf[s, g, lo][:].rearrange("p n j -> p (n j)"), hi - lo)
-            for c in range(lo, hi, COLS):
-                w_mx[s, g, c] = codes[:, c - lo : c - lo + COLS], scales[:, c - lo : c - lo + COLS]
+        def quantise_w(u, first):
+            s, g = UNITS[u][:2]
+            for n, operand in enumerate(quantise("w%d_%d" % (u, first), w_bf[u, first][:])):
+                w_mx[s, g, first + COLS * n] = operand
 
-        def finish(bank, pieces, engine="scalar", queue=nc.sync):
-            place = 0
-            for s, g, lo, hi in pieces:
-                feats = slice(E * g, E * (g + 1))
-                for c in range(lo, hi, COLS):
-                    codes, scales = w_mx[s, g, c]
-                    nc.tensor.matmul_mx(
-                        out=y_banks[bank][:, place, :],
-                        lhsT=codes.bitcast(FP8X4),
-                        lhsT_scale=scales,
-                        rhs=v_codes[:, feats].bitcast(FP8X4),
-                        rhs_scale=v_scales[:, feats],
-                        start=True,
-                        stop=True,
-                    )
-                    place = place + 1
-            return lambda: leave(bank, pieces, place, engine, queue)
+        def values(bank, pieces):
+            chunks = [(s, g, c) for s, g, first, end in pieces for c in range(first, end, COLS)]
+            for n, (s, g, c) in enumerate(chunks):
+                matmul(y_banks[bank][:, n, :], w_mx[s, g, c], v_mx[g], slice(0, P))
 
-        def leave(bank, pieces, count, engine, queue):
-            y_sb = kept("y_sb%d%d_%d" % pieces[0][:3], [P, count, E], F32)
-            if engine == "scalar":
-                nc.scalar.activation(out=y_sb[:], in_=y_banks[bank][:, :count, :], func=ACT.Copy, scale=1.0 / 16.0)
-            else:
-                nc.vector.tensor_scalar(out=y_sb[:], in0=y_banks[bank][:, :count, :], scalar1=1.0 / 16.0, scalar2=None, op0=ALU.mult)
-            place = 0
-            for s, g, lo, hi in pieces:
-                n = (hi - lo) // COLS
-                rows = out[HEAD_SETS[s][g], lo:hi, :]
-                queue.dma_start(out=rows.rearrange("(c m) e -> m c e", m=COLS), in_=y_sb[:, place : place + n, :])
-                place = place + n
+        def store(bank, pieces, divide, queue):
+            count = sum(end - first for s, g, first, end in pieces) // COLS
+            y = sbuf("y%d%d_%d" % pieces[0][:3], [P, count, E], F32)
+            divide(y[:], y_banks[bank][:, :count, :])
+            n = 0
+            for s, g, first, end in pieces:
+                rows = out[HEAD_SETS[s][g], first:end, :].rearrange("(c m) e -> m c e", m=COLS)
+                queue.dma_start(out=rows, in_=y[:, n : n + rows.shape[1], :])
+                n = n + rows.shape[1]
 
-        def load_q3():
-            nc.scalar.dma_start(out=qb_raw[ROWS:], in_=qT[3].rearrange("(p j) n -> p j n", j=PACK))
-            nc.scalar.dma_start(out=v_raw[:], in_=v.rearrange("g (p j) e -> p g j e", j=PACK))
+        def divide_on_scalar(dst, src):
+            nc.scalar.activation(out=dst, in_=src, func=ACT.Copy, scale=1.0 / 16.0)
 
-        t_twice = kept("t_twice", [P, PACK], F32)
-        nc.scalar.dma_start(out=kb_raw[:], in_=kb.rearrange("(p r) o -> p (r o)", r=PACK))
-        nc.scalar.dma_start(out=t_raw[:], in_=t.rearrange("(p r) o -> p (r o)", r=PACK))
+        def divide_on_vector(dst, src):
+            nc.vector.tensor_scalar(out=dst, in0=src, scalar1=1.0 / 16.0, scalar2=None, op0=ALU.mult)
+
+        kb_raw = sbuf("kb_raw", [P, PACK], F32)
+        t_raw = sbuf("t_raw", [P, PACK], F32)
+        k_raw = sbuf("k_raw", [P, PACK, N], F32)
+        q_first = [sbuf("q_first%d" % a, [P, PACK, HALF], F32) for a in range(2)]
+        q_second = sbuf("q_second", [P, PACK, NQ], F32)
+        mask_raw = [sbuf("mask_raw%d" % a, [P, PACK, HALF], F32) for a in range(2)]
+        v_raw = sbuf("v_raw", [P, 2, PACK, E], F32)
+        nc.scalar.dma_start(out=kb_raw[:], in_=kb.rearrange("(s r) o -> s (r o)", r=PACK))
+        nc.scalar.dma_start(out=t_raw[:], in_=t.rearrange("(s r) o -> s (r o)", r=PACK))
         nc.sync.dma_start(out=k_raw[:], in_=kT.rearrange("g (p j) n -> (g p) j n", j=PACK))
-        qa = qT[1:3].rearrange("g (p j) n -> (g p) j n", j=PACK)
-        mask_rows = mask.rearrange("(p r) n -> p r n", r=PACK)
+        q_rows = qT[HEAD_SETS[0][0] : HEAD_SETS[0][1] + 1].rearrange("g (p j) n -> (g p) j n", j=PACK)
+        mask_rows = mask.rearrange("(s r) n -> s r n", r=PACK)
         for a in range(2):
-            nc.sync.dma_start(out=qa_raw[a][:], in_=qa[:, :, HALF * a : HALF * (a + 1)])
+            nc.sync.dma_start(out=q_first[a][:], in_=q_rows[:, :, HALF * a : HALF * (a + 1)])
         nc.sync.dma_start(out=mask_raw[0][:], in_=mask_rows[:, :, :HALF])
-        nc.sync.dma_start(out=qb_raw[:ROWS], in_=qT[0].rearrange("(p j) n -> p j n", j=PACK))
+        nc.sync.dma_start(out=q_second[:ROWS], in_=qT[HEAD_SETS[1][0]].rearrange("(p j) n -> p j n", j=PACK))
         nc.sync.dma_start(out=mask_raw[1][:], in_=mask_rows[:, :, HALF:])
 
-        nc.scalar.activation(out=kb_half[:], in_=kb_raw[:], func=ACT.Copy, scale=0.5)
+        kb_cap = sbuf("kb_cap", [P, PACK], F32)
+        t_cap = sbuf("t_cap", [P, PACK], F32)
+        nc.scalar.activation(out=kb_cap[:], in_=kb_raw[:], func=ACT.Copy, scale=1.0 / CAP)
+
+        k_bf = [sbuf("k_bf%d" % b, [P, 2, COLS, PACK], BF16) for b in range(2)]
         k_src = k_raw[:].rearrange("p j (s b r) -> p b s j r", b=2, r=2)
         nc.vector.tensor_copy(out=k_bf[0][:].rearrange("p r s j -> p s j r"), in_=k_src[:, 0])
         nc.scalar.copy(out=k_bf[1][:].rearrange("p r s j -> p s j r"), in_=k_src[:, 1])
-        nc.vector.tensor_scalar(out=t_twice[:], in0=t_raw[:], scalar1=2.0, scalar2=None, op0=ALU.mult)
-
-        def quantise_k(b):
-            nc.vector.quantize_mx(out=k_codes[b][:].bitcast(FP8X4), scales=k_scales[b][:], in_=k_bf[b][:].rearrange("p r s j -> p (r s j)"))
-
-        quantise_k(0)
-        round_q("vector", 0, 0, 128)
-        round_q("scalar", 0, 128, 256)
-        quantise_k(1)
-        quantise_q(0, 0, 128)
-        quantise_q(0, 128, 256)
+        nc.vector.tensor_scalar(out=t_cap[:], in0=t_raw[:], scalar1=CAP, scalar2=None, op0=ALU.mult)
+        k_mx = quantise("k0", k_bf[0][:].rearrange("p r s j -> p (r s) j"))
+        round_q(nc.vector.tensor_copy, 0, 0, q_first[0][:, :, :COLS])
+        round_q(nc.scalar.copy, 0, COLS, q_first[0][:, :, COLS:])
+        k_mx.extend(quantise("k1", k_bf[1][:].rearrange("p r s j -> p (r s) j")))
+        quantise_q(0, 0)
+        quantise_q(0, COLS)
         scores(0)
-        scores(1, (0, 1))
-        load_q3()
-        round_q("vector", 0, 256, 512)
-        cap(0, (0, 1))
-        scores(1, (2, 3))
+        scores(1)
+
+        nc.scalar.dma_start(out=q_second[ROWS:], in_=qT[HEAD_SETS[1][1]].rearrange("(p j) n -> p j n", j=PACK))
+        nc.scalar.dma_start(out=v_raw[:], in_=v.rearrange("g (s r) e -> s g r e", r=PACK))
+
+        round_q(nc.vector.tensor_copy, 0, HALF, q_first[1][:])
+        cap(0)
+        scale(0)
+        quantise_q(0, HALF)
         scores(2)
-        cap(0, (2, 3))
-        scale(0, (0, 1))
-        quantise_q(0, 256, 512)
-        scale(0, (2, 3))
-        cap(1)
-        scale(1, (0, 1))
-        weigh(0)
-        scale(1, (2, 3))
-        cap(2)
-        scores(3)
-        scores(4)
-        quantise_w(0)
-        weigh(1)
-        scale(2)
-        cap(3)
-        quantise_w(1)
-        weigh(2)
-        cap(4)
-        round_q("scalar", 1, 0, 256)
-        round_q("scalar", 1, 256, 512)
-        scale(3)
-        quantise_w(2)
-        weigh(3)
-        quantise_q(1, 0, 256)
-        scores(5)
-        scale(4)
-        quantise_w(3)
-        quantise_q(1, 256, 512)
-        cap(5)
-        scores(6)
-        scores(7, (0, 1, 2))
-        weigh(4)
-        scale(5)
-        quantise_w(4)
-        cap(6)
-        round_v("scalar")
-        weigh(5)
-        scale(6)
-        quantise_w(5)
-        quantise_v()
-        cap(7, (0,))
-        scores(7, (3,))
-        f0 = finish(0, [(0, 0, 0, 256), (0, 1, 0, 256)])
-        cap(7, (1, 2, 3))
-        f1 = finish(1, [(0, 0, 256, 512), (0, 1, 256, 512)])
-        f0()
-        f1()
-        weigh(6)
-        scale(7)
-        quantise_w(6)
-        finish(0, [(1, 0, 0, 512)])()
-        weigh(7, 0, 256)
-        weigh(7, 256, 384)
-        quantise_w(7, 0, 256)
-        finish(1, [(1, 1, 0, 256)])()
-        weigh(7, 384, 512)
-        quantise_w(7, 256, 384)
-        quantise_w(7, 384, 512)
-        f2 = finish(0, [(1, 1, 256, 384)], "vector")
-        f3 = finish(1, [(1, 1, 384, 512)], "scalar", nc.scalar)
-        f2()
-        f3()
+
+        v_bf = sbuf("v_bf", [P, 2 * E, PACK], BF16)
+        last = len(UNITS) - 1
+        for u in range(last):
+            cap(u + 1)
+            if u + 1 == 2:
+                scores(3)
+            if u + 1 == LAST_OF_FIRST_SET:
+                for first in (0, HALF):
+                    round_q(nc.scalar.copy, 1, first, q_second[:, :, first : first + HALF])
+                nc.scalar.copy(
+                    out=v_bf[:].rearrange("p (g c i) r -> p g c r i", g=2, i=RUN),
+                    in_=v_raw[:].rearrange("p g r (c i) -> p g c r i", i=RUN),
+                )
+            if u + 1 == 6:
+                scores(7)
+                values(0, UNITS[0:3])
+                values(1, UNITS[3:5])
+            if u + 1 == last:
+                store(0, [(0, 0, 0, HALF), UNITS[2]], divide_on_scalar, nc.sync)
+                store(1, UNITS[3:5], divide_on_scalar, nc.sync)
+                values(0, UNITS[5:7])
+                store(0, UNITS[5:7], divide_on_scalar, nc.sync)
+            weigh(u, *UNITS[u][2:])
+            if u + 1 == LAST_OF_FIRST_SET:
+                quantise_q(1, 0)
+                scores(4)
+                scores(5)
+            if u == LAST_OF_FIRST_SET:
+                v_mx = quantise("v", v_bf[:])
+            scale(u + 1)
+            quantise_w(u, UNITS[u][2])
+            if u + 1 == LAST_OF_FIRST_SET:
+                quantise_q(1, HALF)
+                scores(6)
+        values(1, UNITS[7:8])
+        store(1, UNITS[7:8], divide_on_scalar, nc.sync)
+
+        s, g, first, end = UNITS[last]
+        tail = [(s, g, c, c + COLS) for c in range(first, end, COLS)]
+        for piece in tail:
+            weigh(last, *piece[2:])
+        for piece in tail:
+            quantise_w(last, piece[2])
+        for bank, piece in enumerate(tail):
+            values(bank, [piece])
+        store(0, tail[:1], divide_on_vector, nc.sync)
+        store(1, tail[1:], divide_on_scalar, nc.scalar)

from contextlib import ExitStack

import concourse.mybir as mybir

H, D, NQ, N, E = 4, 256, 512, 512, 128
FLOPS = 2 * H * N * NQ * D + 2 * H * NQ * N * E

F32 = mybir.dt.float32
BF16 = mybir.dt.bfloat16
U32 = mybir.dt.uint32
U8 = mybir.dt.uint8
FP8X4 = mybir.dt.float8_e4m3fn_x4
ACT = mybir.ActivationFunctionType
ALU = mybir.AluOpType

P = 128
PACK = 4
ROWS = 64
COLS = 128
HALF = 256
BANK = 512
SCORE_BANKS = 3
RUN = 2
CAP = 2.0

HEAD_SETS = ((1, 2), (0, 3))

UNITS = [(0, 0, 0, COLS), (0, 0, COLS, HALF), (0, 1, 0, HALF), (0, 0, HALF, NQ), (0, 1, HALF, NQ)] + [
    (1, g, first, first + HALF) for first in (0, HALF) for g in range(2)
]
LAST_OF_FIRST_SET = 4


def tile_rows_a_relu_kb_mask_cap_kernel(tc, qT, kT, t, v, kb, mask, out):
    nc = tc.nc
    with ExitStack() as ctx:
        keep = ctx.enter_context(tc.tile_pool(name="keep", bufs=1))
        psum = ctx.enter_context(tc.psum_pool(name="psum", bufs=1))
        ctx.enter_context(tc.manual_schedule())

        def sbuf(name, shape, dtype):
            return keep.tile(shape, dtype, name=name, align_bytes=64)

        score_banks = [[psum.tile([P, BANK], F32, name="score%d%d" % (g, b)) for b in range(SCORE_BANKS)] for g in range(2)]
        y_banks = [psum.tile([P, BANK // E, E], F32, name="y%d" % b) for b in range(2)]

        fills = [[], []]
        score_at = {}
        for u, (s, g, first, end) in enumerate(UNITS):
            width = end - first
            for r in range(PACK):
                column = r * width % BANK
                if column == 0:
                    fills[g].append([])
                bank = score_banks[g][(len(fills[g]) - 1) % SCORE_BANKS]
                score_at[u, r] = bank[:, column : column + width]
                fills[g][-1].extend((u, r, c) for c in range(first, end, COLS))

        q_bf, q_mx, capped, w_bf, w_mx = {}, {}, {}, {}, {}

        def interleave(copy, dst, src):
            copy(out=dst.rearrange("p (c i) j -> p c j i", i=RUN), in_=src.rearrange("p j (c i) -> p c j i", i=RUN))

        def quantise(name, src):
            width = src.shape[1]
            codes = sbuf(name + "_codes", [P, width], U32)
            scales = sbuf(name + "_scales", [P, width], U8)
            nc.vector.quantize_mx(out=codes[:].bitcast(FP8X4), scales=scales[:], in_=src.rearrange("p n j -> p (n j)"))
            return [(codes[:, c : c + COLS], scales[:, c : c + COLS]) for c in range(0, width, COLS)]

        def matmul(dst, stationary, moving, rows):
            nc.tensor.matmul_mx(
                out=dst,
                lhsT=stationary[0][rows].bitcast(FP8X4),
                lhsT_scale=stationary[1][rows],
                rhs=moving[0][rows].bitcast(FP8X4),
                rhs_scale=moving[1][rows],
                start=True,
                stop=True,
            )

        def round_q(copy, s, first, src):
            q_bf[s, first] = sbuf("q_bf%d_%d" % (s, first), [P, src.shape[2], PACK], BF16)
            interleave(copy, q_bf[s, first][:], src)

        def quantise_q(s, first):
            for n, operand in enumerate(quantise("q%d_%d" % (s, first), q_bf[s, first][:])):
                q_mx[s, first + COLS * n] = operand

        def scores(n):
            for calls in zip(fills[0][n], fills[1][n]):
                for u, r, c in calls:
                    s, g, first, end = UNITS[u]
                    dst = score_at[u, r][:, c - first : c - first + COLS]
                    matmul(dst, k_mx[r], q_mx[s, c], slice(ROWS * g, ROWS * (g + 1)))

        def cap(u):
            s, g, first, end = UNITS[u]
            capped[u] = sbuf("capped%d" % u, [P, PACK, end - first], F32)
            for r in range(PACK):
                nc.scalar.activation(
                    out=capped[u][:, r, :], in_=score_at[u, r], func=ACT.Tanh, bias=kb_cap[:, r : r + 1], scale=1.0 / CAP
                )

        def scale(u):
            for r in range(PACK):
                row = capped[u][:, r, :]
                nc.vector.tensor_scalar(out=row, in0=row, scalar1=0.0, scalar2=t_cap[:, r : r + 1], op0=ALU.max, op1=ALU.mult)

        def weigh(u, first, end):
            offset = first - UNITS[u][2]
            seen = mask_raw[first // HALF][:, :, first % HALF : first % HALF + end - first]
            w_bf[u, first] = sbuf("w_bf%d_%d" % (u, first), [P, end - first, PACK], BF16)
            nc.vector.tensor_tensor(
                out=w_bf[u, first][:].rearrange("p (c i) r -> p c r i", i=RUN),
                in0=capped[u][:, :, offset : offset + end - first].rearrange("p r (c i) -> p c r i", i=RUN),
                in1=seen.rearrange("p r (c i) -> p c r i", i=RUN),
                op=ALU.mult,
            )

        def quantise_w(u, first):
            s, g = UNITS[u][:2]
            for n, operand in enumerate(quantise("w%d_%d" % (u, first), w_bf[u, first][:])):
                w_mx[s, g, first + COLS * n] = operand

        def values(bank, pieces):
            chunks = [(s, g, c) for s, g, first, end in pieces for c in range(first, end, COLS)]
            for n, (s, g, c) in enumerate(chunks):
                matmul(y_banks[bank][:, n, :], w_mx[s, g, c], v_mx[g], slice(0, P))

        def store(bank, pieces, divide, queue):
            count = sum(end - first for s, g, first, end in pieces) // COLS
            y = sbuf("y%d%d_%d" % pieces[0][:3], [P, count, E], F32)
            divide(y[:], y_banks[bank][:, :count, :])
            n = 0
            for s, g, first, end in pieces:
                rows = out[HEAD_SETS[s][g], first:end, :].rearrange("(c m) e -> m c e", m=COLS)
                queue.dma_start(out=rows, in_=y[:, n : n + rows.shape[1], :])
                n = n + rows.shape[1]

        def divide_on_scalar(dst, src):
            nc.scalar.activation(out=dst, in_=src, func=ACT.Copy, scale=1.0 / 16.0)

        def divide_on_vector(dst, src):
            nc.vector.tensor_scalar(out=dst, in0=src, scalar1=1.0 / 16.0, scalar2=None, op0=ALU.mult)

        kb_raw = sbuf("kb_raw", [P, PACK], F32)
        t_raw = sbuf("t_raw", [P, PACK], F32)
        k_raw = sbuf("k_raw", [P, PACK, N], F32)
        q_first = [sbuf("q_first%d" % a, [P, PACK, HALF], F32) for a in range(2)]
        q_second = sbuf("q_second", [P, PACK, NQ], F32)
        mask_raw = [sbuf("mask_raw%d" % a, [P, PACK, HALF], F32) for a in range(2)]
        v_raw = sbuf("v_raw", [P, 2, PACK, E], F32)
        nc.scalar.dma_start(out=kb_raw[:], in_=kb.rearrange("(s r) o -> s (r o)", r=PACK))
        nc.scalar.dma_start(out=t_raw[:], in_=t.rearrange("(s r) o -> s (r o)", r=PACK))
        nc.sync.dma_start(out=k_raw[:], in_=kT.rearrange("g (p j) n -> (g p) j n", j=PACK))
        q_rows = qT[HEAD_SETS[0][0] : HEAD_SETS[0][1] + 1].rearrange("g (p j) n -> (g p) j n", j=PACK)
        mask_rows = mask.rearrange("(s r) n -> s r n", r=PACK)
        for a in range(2):
            nc.sync.dma_start(out=q_first[a][:], in_=q_rows[:, :, HALF * a : HALF * (a + 1)])
        nc.sync.dma_start(out=mask_raw[0][:], in_=mask_rows[:, :, :HALF])
        nc.sync.dma_start(out=q_second[:ROWS], in_=qT[HEAD_SETS[1][0]].rearrange("(p j) n -> p j n", j=PACK))
        nc.sync.dma_start(out=mask_raw[1][:], in_=mask_rows[:, :, HALF:])

        kb_cap = sbuf("kb_cap", [P, PACK], F32)
        t_cap = sbuf("t_cap", [P, PACK], F32)
        nc.scalar.activation(out=kb_cap[:], in_=kb_raw[:], func=ACT.Copy, scale=1.0 / CAP)

        k_bf = [sbuf("k_bf%d" % b, [P, 2, COLS, PACK], BF16) for b in range(2)]
        k_src = k_raw[:].rearrange("p j (s b r) -> p b s j r", b=2, r=2)
        nc.vector.tensor_copy(out=k_bf[0][:].rearrange("p r s j -> p s j r"), in_=k_src[:, 0])
        nc.scalar.copy(out=k_bf[1][:].rearrange("p r s j -> p s j r"), in_=k_src[:, 1])
        nc.vector.tensor_scalar(out=t_cap[:], in0=t_raw[:], scalar1=CAP, scalar2=None, op0=ALU.mult)
        k_mx = quantise("k0", k_bf[0][:].rearrange("p r s j -> p (r s) j"))
        round_q(nc.vector.tensor_copy, 0, 0, q_first[0][:, :, :COLS])
        round_q(nc.scalar.copy, 0, COLS, q_first[0][:, :, COLS:])
        k_mx.extend(quantise("k1", k_bf[1][:].rearrange("p r s j -> p (r s) j")))
        quantise_q(0, 0)
        quantise_q(0, COLS)
        scores(0)
        scores(1)

        nc.scalar.dma_start(out=q_second[ROWS:], in_=qT[HEAD_SETS[1][1]].rearrange("(p j) n -> p j n", j=PACK))
        nc.scalar.dma_start(out=v_raw[:], in_=v.rearrange("g (s r) e -> s g r e", r=PACK))

        round_q(nc.vector.tensor_copy, 0, HALF, q_first[1][:])
        cap(0)
        scale(0)
        quantise_q(0, HALF)
        scores(2)

        v_bf = sbuf("v_bf", [P, 2 * E, PACK], BF16)
        last = len(UNITS) - 1
        for u in range(last):
            cap(u + 1)
            if u + 1 == 2:
                scores(3)
            if u + 1 == LAST_OF_FIRST_SET:
                for first in (0, HALF):
                    round_q(nc.scalar.copy, 1, first, q_second[:, :, first : first + HALF])
                nc.scalar.copy(
                    out=v_bf[:].rearrange("p (g c i) r -> p g c r i", g=2, i=RUN),
                    in_=v_raw[:].rearrange("p g r (c i) -> p g c r i", i=RUN),
                )
            if u + 1 == 6:
                scores(7)
                values(0, UNITS[0:3])
                values(1, UNITS[3:5])
            if u + 1 == last:
                store(0, [(0, 0, 0, HALF), UNITS[2]], divide_on_scalar, nc.sync)
                store(1, UNITS[3:5], divide_on_scalar, nc.sync)
                values(0, UNITS[5:7])
                store(0, UNITS[5:7], divide_on_scalar, nc.sync)
            weigh(u, *UNITS[u][2:])
            if u + 1 == LAST_OF_FIRST_SET:
                quantise_q(1, 0)
                scores(4)
                scores(5)
            if u == LAST_OF_FIRST_SET:
                v_mx = quantise("v", v_bf[:])
            scale(u + 1)
            quantise_w(u, UNITS[u][2])
            if u + 1 == LAST_OF_FIRST_SET:
                quantise_q(1, HALF)
                scores(6)
        values(1, UNITS[7:8])
        store(1, UNITS[7:8], divide_on_scalar, nc.sync)

        s, g, first, end = UNITS[last]
        tail = [(s, g, c, c + COLS) for c in range(first, end, COLS)]
        for piece in tail:
            weigh(last, *piece[2:])
        for piece in tail:
            quantise_w(last, piece[2])
        for bank, piece in enumerate(tail):
            values(bank, [piece])
        store(0, tail[:1], divide_on_vector, nc.sync)
        store(1, tail[1:], divide_on_scalar, nc.scalar)
